import numpy as np
import ml_dtypes


def mxq(x, axis, fmt="e4m3"):
    dtype, down = {"e4m3": (ml_dtypes.float8_e4m3fn, 7), "e5m2": (ml_dtypes.float8_e5m2, 14)}[fmt]
    v = np.moveaxis(np.asarray(x, np.float32).astype(ml_dtypes.bfloat16).astype(np.float64), axis, -1)
    blocks = v.reshape(v.shape[:-1] + (-1, 32))
    amax = np.abs(blocks).max(-1, keepdims=True)
    byte = np.maximum(np.where(amax > 0, np.frexp(amax)[1] - 1 + 127, 0) - down, 1)
    scale = np.exp2(byte - 127.0)
    codes = (blocks / scale).astype(np.float32).astype(dtype).astype(np.float64)
    return np.moveaxis((codes * scale).reshape(v.shape), -1, axis)


WIDE = False


def mx_kscale(k):
    if not WIDE:
        return np.ones(k)
    levels = np.array([10, -10, 5, -5, 0])
    if k % 512:
        return np.exp2(np.random.permutation(np.resize(levels, k // 32))).repeat(32)
    a = np.empty((k // 512, 16))
    for p in range(k // 512):
        a[p, :8] = np.random.permutation(np.resize(levels, 8))
        for g in range(8):
            far = levels[np.abs(levels - a[p, g]) >= 10]
            a[p, g + 8] = far[np.random.randint(len(far))]
    return np.exp2(a.ravel()).repeat(32)


def f64(x):
    return np.asarray(x).astype(np.float64)


def striped(idx):
    return np.tile(idx.reshape(-1, 16).T, (8, 1)).astype(np.uint16)


def unstriped(offs):
    return offs[:16].T.reshape(-1).astype(np.int64)


def striped8(idx):
    return np.concatenate([x.reshape(-1, 16).T for x in idx]).astype(np.uint16)


def runs(offs, k):
    lists = np.stack([offs[16 * r : 16 * r + 16].T.reshape(-1) for r in range(8)]).astype(np.int64)
    return lists[np.arange(k) % 512 // 64]


def pack_weight(w):
    k, n = w.shape
    w = f64(np.asarray(w, np.float32).astype(ml_dtypes.bfloat16)).reshape(k // 32, 32, n)
    amax = np.abs(w).max(1)
    byte = np.clip(np.where(amax > 0, np.frexp(amax)[1] - 1 + 127 - 7, 1), 1, 254)
    scaled = (w * np.exp2(127.0 - byte)[:, None, :]).reshape(k, n).astype(np.float32)
    words = np.ascontiguousarray(scaled.reshape(k // 512, 128, 4, n).transpose(0, 1, 3, 2)).astype(ml_dtypes.float8_e4m3fn).view(np.uint8)
    return words, np.ascontiguousarray(byte.astype(np.uint8).reshape(k // 512, 16, n))


def unpack_weight(words, scales):
    g, p, n, _ = words.shape
    vals = np.ascontiguousarray(words).view(ml_dtypes.float8_e4m3fn).astype(np.float64) * np.repeat(np.exp2(scales.astype(np.float64) - 127.0), 8, axis=1)[..., None]
    return vals.transpose(0, 1, 3, 2).reshape(g * 512, n)


K, T, S, N, G, H, W, U = 512, 1024, 256, 512, 2048, 512, 128, 1024


def setup_inputs():
    n = np.random.standard_normal
    s = mx_kscale(K)[:, None]
    u = mx_kscale(K)
    packed_xT = pack_weight(n((K, T)) * s)
    packed_dT = pack_weight(n((K, G)) / s)
    perm = np.random.permutation(S)
    return {
        "x_words": packed_xT[0],
        "x_scales": packed_xT[1],
        "d_words": packed_dT[0],
        "d_scales": packed_dT[1],
        "gn": (np.random.uniform(0.5, 1.5, (H, 1)) * u[:, None]).astype(np.float32),
        "gm": (np.random.uniform(0.5, 1.5, (H, 1)) * u[:, None]).astype(np.float32),
        "w1": (n((H, N)) / np.sqrt(2 * H) / u[:, None]).astype(np.float32),
        "w2": (n((H, N)) / np.sqrt(2 * H) / u[:, None]).astype(np.float32),
        "offs": striped(np.random.permutation(T)[:S]),
        "k1": striped8(np.random.randint(0, G, (8, H))),
        "two": striped(np.random.permutation(T)[:S]),
        "k2": striped8(np.random.randint(0, G, (8, H))),
        "n1": striped(perm[:W]),
        "n2": striped(perm[W:]),
        "n3": striped8(np.stack([np.random.permutation(S) for _ in range(8)])),
        "n4": striped8(np.stack([np.random.permutation(S) for _ in range(8)])),
        "n5": striped(np.random.randint(0, S, U)),
    }


def reference(x_words, x_scales, d_words, d_scales, gn, gm, w1, w2, offs, k1, two, k2, n1, n2, n3, n4, n5):
    d_k1 = unpack_weight(d_words, d_scales)[np.arange(K)[:, None], runs(k1, K)]
    xq = unpack_weight(x_words, x_scales)[:, unstriped(offs)]
    a = 0.0625 * (d_k1.T @ xq)
    pa = a[:, unstriped(n1)]
    pb = a[:, unstriped(n2)]
    rb = np.maximum(pa, pb)
    ra = pa / (np.abs(pb) + 0.5)
    ds = np.zeros((H, S))
    ds[:, unstriped(n1)] = ra
    dt = ds.copy()
    dt[:, unstriped(n2)] = rb
    z = f64(gn) * dt
    d_k2 = unpack_weight(d_words, d_scales)[np.arange(K)[:, None], runs(k2, K)]
    x_two = unpack_weight(x_words, x_scales)[:, unstriped(two)]
    b = 0.0625 * (d_k2.T @ x_two)
    pa2 = b[np.arange(H)[:, None], runs(n3, H)]
    pb2 = b[np.arange(H)[:, None], runs(n4, H)]
    mu = 0.3125 * (b + pa2 + pb2)
    z2 = f64(gm) * ((b - mu) / (np.sqrt((pa2 - mu) ** 2 + (pb2 - mu) ** 2 + 0.25)))
    h = mxq(f64(w1), 0, "e4m3").T @ mxq(z, 0, "e4m3") + mxq(f64(w2), 0, "e4m3").T @ mxq(z2, 0, "e4m3")
    mb = h[:, unstriped(n5)]
    mx = mb.reshape(N, S, 4).max(axis=2)
    return h - mx

@@ -1,0 +1,302 @@
+from contextlib import ExitStack
+
+import concourse.mybir as mybir
+
+K, T, S, N, G, H, W, U = 512, 1024, 256, 512, 2048, 512, 128, 1024
+FLOPS = 4 * 2 * 512 * 512 * 256
+
+F32 = mybir.dt.float32
+BF16 = mybir.dt.bfloat16
+I32 = mybir.dt.int32
+U32 = mybir.dt.uint32
+U16 = mybir.dt.uint16
+U8 = mybir.dt.uint8
+FP8X4 = mybir.dt.float8_e4m3fn_x4
+ALU = mybir.AluOpType
+ACT = mybir.ActivationFunctionType
+
+P = 128
+PACK = 4
+B_WIN = 512
+H_WIN = 528
+H_PIECE = 512
+
+
+def tile_picked_pqjratiostdgmaxd_none_p_kernel(
+    tc, x_words, x_scales, d_words, d_scales, gn, gm, w1, w2, offs, k1, two, k2, n1, n2, n3, n4, n5, out
+):
+    nc = tc.nc
+    with ExitStack() as ctx:
+        keep = ctx.enter_context(tc.tile_pool(name="keep", bufs=1))
+        psum = ctx.enter_context(tc.psum_pool(name="psum", bufs=1))
+
+        def sb(name, shape, dtype):
+            return keep.tile(shape, dtype, name=name, align_bytes=64)
+
+        def load_list(name, src):
+            tile = keep.tile(list(src.shape), U16, name=name)
+            nc.sync.dma_start(tile[:], src)
+            return tile
+
+        def load_scale_rows(name, src, width):
+            tile = sb(name, [P, width], U8)
+            rows = src[0].bitcast(I32).rearrange("(r e) c -> e r c", e=2)
+            for e in range(2):
+                nc.sync.dma_start(
+                    tile[e:P:2, :].bitcast(I32), rows[e].unsqueeze(1).to_broadcast([8, 8, width // 4])
+                )
+            return tile
+
+        def load_words(name, src, width):
+            tile = sb(name, [P, width], I32)
+            nc.sync.dma_start(tile[:], src[0].rearrange("p n t -> p (n t)").bitcast(I32))
+            return tile
+
+        k2_t = load_list("k2_t", k2)
+        d_sc = load_scale_rows("d_sc", d_scales, G)
+        two_t = load_list("two_t", two)
+        x_sc = load_scale_rows("x_sc", x_scales, T)
+        d_wd = load_words("d_wd", d_words, G)
+        n3_t = load_list("n3_t", n3)
+        x_wd = load_words("x_wd", x_words, T)
+        k1_t = load_list("k1_t", k1)
+        offs_t = load_list("offs_t", offs)
+        n4_t = load_list("n4_t", n4)
+        n1_t = load_list("n1_t", n1)
+        n2_t = load_list("n2_t", n2)
+        n5_t = load_list("n5_t", n5)
+
+        b_win = [sb("b_win%d" % t, [P, B_WIN], F32) for t in range(PACK)]
+        h_win = [sb("h_win%d" % m, [P, H_WIN], F32) for m in range(N // P)]
+        for t in range(PACK):
+            nc.gpsimd.memset(b_win[t][:, S:], 0.0)
+        gm_raw = sb("gm_raw", [P, PACK], F32)
+        nc.gpsimd.dma_start(gm_raw[:], gm.rearrange("(p t) o -> p (t o)", t=PACK))
+        gn_t = sb("gn_t", [P, PACK], F32)
+        nc.gpsimd.dma_start(gn_t[:], gn.rearrange("(p t) o -> p (t o)", t=PACK))
+        for m in range(N // P):
+            nc.gpsimd.memset(h_win[m][:, S:], 0.0)
+        gm_t = sb("gm_t", [P, PACK], F32)
+        nc.gpsimd.tensor_scalar(gm_t[:], gm_raw[:], 0.6875 / 16, 0.0, ALU.mult, ALU.add)
+
+        def coded_product(name, k_list, x_list, queue):
+            d_bytes = sb("d_bytes_" + name, [P, H], U8)
+            nc.vector.tensor_copy(d_bytes[:], d_sc[:].indirect(k_list[:]))
+            x_bytes = sb("x_bytes_" + name, [P, S], U8)
+            nc.vector.tensor_copy(x_bytes[:], x_sc[:].indirect(x_list[:]))
+            plane = sb("plane_" + name, [P, H + S], U8)
+            nc.vector.tensor_copy(
+                plane[:, :H].rearrange("p (t m) -> p m t", t=PACK), d_bytes[:].rearrange("p (m t) -> p m t", t=PACK)
+            )
+            nc.vector.tensor_copy(plane[:, H:].bitcast(I32), x_bytes[:].bitcast(I32))
+            for e in range(2):
+                queue.dma_start(plane[2 + e : P : 32, :].bitcast(I32), plane[16 + e : P : 32, :].bitcast(I32))
+
+            d_codes = sb("d_codes_" + name, [P, H], U32)
+            nc.vector.tensor_copy(d_codes[:], d_wd[:].bitcast(U32).indirect(k_list[:]))
+            x_codes = sb("x_codes_" + name, [P, S], U32)
+            nc.vector.tensor_copy(x_codes[:], x_wd[:].bitcast(U32).indirect(x_list[:]))
+            dealt = sb("dealt_" + name, [P, H], U32)
+            nc.vector.tensor_copy(
+                dealt[:].bitcast(I32).rearrange("p (t c i) -> p c t i", t=PACK, i=4),
+                d_codes[:].bitcast(I32).rearrange("p (c i t) -> p c t i", t=PACK, i=4),
+            )
+            banks = []
+            for pair in range(2):
+                bank = psum.tile([P, 2, S], F32, name="bank_%s%d" % (name, pair))
+                for u in range(2):
+                    cols = slice((2 * pair + u) * P, (2 * pair + u + 1) * P)
+                    nc.tensor.matmul_mx(
+                        out=bank[:, u, :],
+                        lhsT=dealt[:, cols].bitcast(FP8X4),
+                        lhsT_scale=plane[:, cols],
+                        rhs=x_codes[:].bitcast(FP8X4),
+                        rhs_scale=plane[:, H:],
+                        start=True,
+                        stop=True,
+                    )
+                banks.append(bank)
+            return banks
+
+        b_banks = coded_product("b", k2_t, two_t, nc.scalar)
+
+        pa2 = [sb("pa2_%d" % pair, [P, 2, S], F32) for pair in range(2)]
+        pb2 = [sb("pb2_%d" % pair, [P, 2, S], F32) for pair in range(2)]
+        for t in range(PACK):
+            pair, u = divmod(t, 2)
+            nc.scalar.activation(b_win[t][:, :S], b_banks[pair][:, u, :], ACT.Copy, scale=0.0625)
+            nc.scalar.activation(pa2[pair][:, u, :], b_win[t][:].indirect(n3_t[:]), ACT.Copy)
+            nc.scalar.activation(pb2[pair][:, u, :], b_win[t][:].indirect(n4_t[:]), ACT.Copy)
+
+        a_banks = coded_product("a", k1_t, offs_t, nc.sync)
+
+        w_raw = {}
+        for name, src in (("w2", w2), ("w1", w1)):
+            w_raw[name] = sb(name + "_raw", [P, PACK, N], F32)
+            nc.sync.dma_start(w_raw[name][:], src.rearrange("(p t) m -> p t m", t=PACK))
+
+        z_grouped = sb("z_grouped", [P, S, PACK], BF16)
+        z2_planes = sb("z2_planes", [P, PACK, S], BF16)
+        offset = {}
+        inv = {}
+
+        work = {}
+
+        def b_tile(name, pair):
+            work[name, pair] = sb("%s_%d" % (name, pair), [P, 2, S], F32)
+            return work[name, pair][:]
+
+        def b_sums(pair):
+            nc.vector.tensor_tensor(b_tile("s1", pair), pa2[pair][:], pb2[pair][:], ALU.add)
+            nc.vector.tensor_tensor(b_tile("dd", pair), pa2[pair][:], pb2[pair][:], ALU.subtract)
+
+        def b_middle(pair):
+            s1, dd = work["s1", pair][:], work["dd", pair][:]
+            nc.vector.scalar_tensor_tensor(b_tile("ee", pair), s1, -9.6, b_banks[pair][:], ALU.mult, ALU.add)
+            nc.vector.tensor_tensor(b_tile("dd2", pair), dd, dd, ALU.mult)
+
+        def b_spread(pair):
+            s1, ee = work["s1", pair][:], work["ee", pair][:]
+            nc.vector.scalar_tensor_tensor(b_tile("ee2", pair), ee, (0.625 / 16) ** 2, ee, ALU.mult, ALU.mult)
+            offset[pair] = b_tile("offset", pair)
+            nc.vector.scalar_tensor_tensor(offset[pair], s1, -80.0 / 11.0, b_banks[pair][:], ALU.mult, ALU.add)
+            spread = b_tile("spread", pair)
+            nc.vector.tensor_tensor(spread, work["dd2", pair][:], work["ee2", pair][:], ALU.add)
+            inv[pair] = b_tile("inv", pair)
+            nc.scalar.activation(inv[pair], spread, ACT.Abs_reciprocal_sqrt, bias=0.25, scale=0.5)
+
+        def b_finish(pair):
+            for u in range(2):
+                t = 2 * pair + u
+                nc.vector.scalar_tensor_tensor(
+                    z2_planes[:, t, :], offset[pair][:, u, :], gm_t[:, t : t + 1], inv[pair][:, u, :], ALU.mult, ALU.mult
+                )
+
+        pa = [sb("pa_%d" % pair, [P, 2, W], F32) for pair in range(2)]
+        pb = [sb("pb_%d" % pair, [P, 2, W], F32) for pair in range(2)]
+        dt = [sb("dt_%d" % t, [P, S], F32) for t in range(PACK)]
+        root = {}
+
+        def a_fetch(pair):
+            for u in range(2):
+                t = 2 * pair + u
+                a_win = sb("a_win%d" % t, [P, S], F32)
+                nc.vector.tensor_scalar(a_win[:], a_banks[pair][:, u, :], 0.0625, None, ALU.mult)
+                nc.scalar.activation(pb[pair][:, u, :], a_win[:].indirect(n2_t[:]), ACT.Copy)
+                nc.scalar.activation(pa[pair][:, u, :], a_win[:].indirect(n1_t[:]), ACT.Copy)
+
+        def a_larger(pair):
+            size = sb("size_%d" % pair, [P, 2, W], F32)
+            nc.vector.scalar_tensor_tensor(size[:], pb[pair][:], -1.0, pb[pair][:], ALU.mult, ALU.max)
+            rb = sb("rb_%d" % pair, [P, 2, W], F32)
+            nc.vector.tensor_tensor(rb[:], pa[pair][:], pb[pair][:], ALU.max)
+            root[pair] = sb("root_%d" % pair, [P, 2, W], F32)
+            nc.scalar.activation(root[pair][:], size[:], ACT.Abs_reciprocal_sqrt, bias=0.5)
+            for u in range(2):
+                nc.scalar.activation(dt[2 * pair + u][:].indirect(n2_t[:]), rb[:, u, :], ACT.Copy)
+
+        def a_ratio(pair):
+            half = sb("half_%d" % pair, [P, 2, W], F32)
+            nc.vector.tensor_tensor(half[:], pa[pair][:], root[pair][:], ALU.mult)
+            ra = sb("ra_%d" % pair, [P, 2, W], F32)
+            nc.vector.tensor_tensor(ra[:], half[:], root[pair][:], ALU.mult)
+            for u in range(2):
+                nc.scalar.activation(dt[2 * pair + u][:].indirect(n1_t[:]), ra[:, u, :], ACT.Copy)
+
+        def a_round(pair):
+            for u in range(2):
+                t = 2 * pair + u
+                nc.vector.tensor_scalar(z_grouped[:, :, t], dt[t][:], gn_t[:, t : t + 1], None, ALU.mult)
+
+        def quantize(name, grouped, width):
+            codes = sb(name + "_codes", [P, width], U32)
+            scales = sb(name + "_scales", [P, width], U8)
+            nc.vector.quantize_mx(
+                out=codes[:].bitcast(FP8X4), scales=scales[:], in_=grouped[:].rearrange("p w t -> p (w t)")
+            )
+            return codes, scales
+
+        def interleave(name, src, width):
+            grouped = sb(name + "_grouped", [P, width, PACK], BF16)
+            nc.vector.tensor_copy(
+                grouped[:].rearrange("p (c i) t -> p c t i", i=4), src.rearrange("p t (c i) -> p c t i", i=4)
+            )
+            return grouped
+
+        wq = {}
+
+        def weights(m):
+            cols = slice(m * P, (m + 1) * P)
+            grouped = {name: interleave("%s_%d" % (name, m), w_raw[name][:, :, cols], P) for name in ("w2", "w1")}
+            for name in ("w2", "w1"):
+                wq[name, m] = quantize("%s_%d" % (name, m), grouped[name], P)
+
+        b_sums(0)
+        a_fetch(0)
+        b_middle(0)
+        a_fetch(1)
+        b_spread(0)
+        b_sums(1)
+        a_larger(0)
+        b_middle(1)
+        a_larger(1)
+        b_spread(1)
+        a_ratio(0)
+        a_ratio(1)
+        b_finish(0)
+        weights(0)
+        b_finish(1)
+        z2_grouped = interleave("z2", z2_planes[:], S)
+        a_round(0)
+        z2q = quantize("z2", z2_grouped, S)
+        a_round(1)
+        zq = quantize("z", z_grouped, S)
+
+        def h_product(m):
+            bank = psum.tile([P, S], F32, name="bank_h%d" % m)
+            for first, name, act in ((True, "w2", z2q), (False, "w1", zq)):
+                nc.tensor.matmul_mx(
+                    out=bank[:],
+                    lhsT=wq[name, m][0][:].bitcast(FP8X4),
+                    lhsT_scale=wq[name, m][1][:],
+                    rhs=act[0][:].bitcast(FP8X4),
+                    rhs_scale=act[1][:],
+                    start=first,
+                    stop=not first,
+                )
+            nc.vector.tensor_copy(h_win[m][:, :S], bank[:])
+
+        def h_finish(m, first, count, result):
+            tag = "%d_%d" % (m, first)
+            cols = slice(first // 4, (first + count) // 4)
+            members = sb("members_" + tag, [P, count // 4, 4], F32)
+            nc.scalar.activation(
+                members[:].rearrange("p j t -> p (j t)"),
+                h_win[m][:].indirect(n5_t[:, first // 16 : (first + count) // 16]),
+                ACT.Copy,
+            )
+            largest = sb("largest_" + tag, [P, count // 4], F32)
+            if count == H_PIECE:
+                pairs = sb("pairs_" + tag, [P, count // 4, 2], F32)
+                nc.vector.tensor_tensor(pairs[:], members[:, :, 0:2], members[:, :, 2:4], ALU.max)
+                nc.vector.tensor_tensor(largest[:], pairs[:, :, 0], pairs[:, :, 1], ALU.max)
+            else:
+                nc.vector.tensor_reduce(largest[:], members[:], mybir.AxisListType.X, ALU.max)
+            nc.vector.tensor_tensor(result[:, cols], h_win[m][:, cols], largest[:], ALU.subtract)
+
+        h_product(0)
+        for m in range(1, N // P):
+            weights(m)
+            h_product(m)
+        for m in range(N // P):
+            rows = slice(m * P, (m + 1) * P)
+            result = sb("result_%d" % m, [P, S], F32)
+            if m + 1 < N // P:
+                for first in range(0, U, H_PIECE):
+                    h_finish(m, first, H_PIECE, result)
+                nc.sync.dma_start(out[rows, :], result[:])
+            else:
+                for first, count in ((0, 512), (512, 256), (768, 256)):
+                    h_finish(m, first, count, result)
+                    cols = slice(first // 4, (first + count) // 4)
+                    nc.sync.dma_start(out[rows, cols], result[:, cols])

@@ -15,6 +15,9 @@ FP8X4 = mybir.dt.float8_e4m3fn_x4
 ALU = mybir.AluOpType
 ACT = mybir.ActivationFunctionType
 
+BS = 4
+AS = 2
+LAST = ((0, 448), (448, 384), (832, 192))
 P = 128
 PACK = 4
 B_WIN = 512
@@ -30,8 +33,8 @@ def tile_picked_pqjratiostdgmaxd_none_p_kernel(
         keep = ctx.enter_context(tc.tile_pool(name="keep", bufs=1))
         psum = ctx.enter_context(tc.psum_pool(name="psum", bufs=1))
 
-        def sb(name, shape, dtype):
-            return keep.tile(shape, dtype, name=name, align_bytes=64)
+        def sb(name, shape, dtype, tag=""):
+            return keep.tile(shape, dtype, name=name, tag=tag or name, align_bytes=64)
 
         def load_list(name, src):
             tile = keep.tile(list(src.shape), U16, name=name)
@@ -40,11 +43,13 @@ def tile_picked_pqjratiostdgmaxd_none_p_kernel(
 
         def load_scale_rows(name, src, width):
             tile = sb(name, [P, width], U8)
-            rows = src[0].bitcast(I32).rearrange("(r e) c -> e r c", e=2)
-            for e in range(2):
-                nc.sync.dma_start(
-                    tile[e:P:2, :].bitcast(I32), rows[e].unsqueeze(1).to_broadcast([8, 8, width // 4])
-                )
+            rows = src[0].bitcast(I32)
+            nc.sync.dma_start(tile[:].bitcast(I32), rows.unsqueeze(1).to_broadcast([16, 8, width // 4]))
+            return tile
+
+        def load_gains(name, src, slot):
+            tile = sb(name, [P, PACK], F32, tag=slot)
+            nc.sync.dma_start(tile[:], src.rearrange("(p t) o -> p (t o)", t=PACK))
             return tile
 
         def load_words(name, src, width):
@@ -56,28 +61,23 @@ def tile_picked_pqjratiostdgmaxd_none_p_kernel(
         d_sc = load_scale_rows("d_sc", d_scales, G)
         two_t = load_list("two_t", two)
         x_sc = load_scale_rows("x_sc", x_scales, T)
-        d_wd = load_words("d_wd", d_words, G)
         n3_t = load_list("n3_t", n3)
+        n4_t = load_list("n4_t", n4)
+        n1_t = load_list("n1_t", n1)
+        d_wd = load_words("d_wd", d_words, G)
         x_wd = load_words("x_wd", x_words, T)
         k1_t = load_list("k1_t", k1)
         offs_t = load_list("offs_t", offs)
-        n4_t = load_list("n4_t", n4)
-        n1_t = load_list("n1_t", n1)
         n2_t = load_list("n2_t", n2)
         n5_t = load_list("n5_t", n5)
 
+        warm_in = sb("warm_in", [P, 1], F32)
+        nc.vector.memset(warm_in[:], 1.0)
+        warm_out = sb("warm_out", [P, 1], F32)
+        nc.scalar.activation(warm_out[:], warm_in[:], ACT.Abs_reciprocal_sqrt, bias=0.25, scale=0.5)
+
         b_win = [sb("b_win%d" % t, [P, B_WIN], F32) for t in range(PACK)]
         h_win = [sb("h_win%d" % m, [P, H_WIN], F32) for m in range(N // P)]
-        for t in range(PACK):
-            nc.gpsimd.memset(b_win[t][:, S:], 0.0)
-        gm_raw = sb("gm_raw", [P, PACK], F32)
-        nc.gpsimd.dma_start(gm_raw[:], gm.rearrange("(p t) o -> p (t o)", t=PACK))
-        gn_t = sb("gn_t", [P, PACK], F32)
-        nc.gpsimd.dma_start(gn_t[:], gn.rearrange("(p t) o -> p (t o)", t=PACK))
-        for m in range(N // P):
-            nc.gpsimd.memset(h_win[m][:, S:], 0.0)
-        gm_t = sb("gm_t", [P, PACK], F32)
-        nc.gpsimd.tensor_scalar(gm_t[:], gm_raw[:], 0.6875 / 16, 0.0, ALU.mult, ALU.add)
 
         def coded_product(name, k_list, x_list, queue):
             d_bytes = sb("d_bytes_" + name, [P, H], U8)
@@ -89,8 +89,8 @@ def tile_picked_pqjratiostdgmaxd_none_p_kernel(
                 plane[:, :H].rearrange("p (t m) -> p m t", t=PACK), d_bytes[:].rearrange("p (m t) -> p m t", t=PACK)
             )
             nc.vector.tensor_copy(plane[:, H:].bitcast(I32), x_bytes[:].bitcast(I32))
-            for e in range(2):
-                queue.dma_start(plane[2 + e : P : 32, :].bitcast(I32), plane[16 + e : P : 32, :].bitcast(I32))
+            for c in range(1, 4):
+                queue.dma_start(plane[c:P:32, :].bitcast(I32), plane[8 * c : P : 32, :].bitcast(I32))
 
             d_codes = sb("d_codes_" + name, [P, H], U32)
             nc.vector.tensor_copy(d_codes[:], d_wd[:].bitcast(U32).indirect(k_list[:]))
@@ -120,19 +120,25 @@ def tile_picked_pqjratiostdgmaxd_none_p_kernel(
 
         b_banks = coded_product("b", k2_t, two_t, nc.scalar)
 
+        gm_t = load_gains("gm_t", gm, "x_codes_b")
+        gn_t = load_gains("gn_t", gn, "dealt_b")
+
         pa2 = [sb("pa2_%d" % pair, [P, 2, S], F32) for pair in range(2)]
         pb2 = [sb("pb2_%d" % pair, [P, 2, S], F32) for pair in range(2)]
         for t in range(PACK):
             pair, u = divmod(t, 2)
-            nc.scalar.activation(b_win[t][:, :S], b_banks[pair][:, u, :], ACT.Copy, scale=0.0625)
+            if t < BS:
+                nc.scalar.activation(b_win[t][:, :S], b_banks[pair][:, u, :], ACT.Copy, scale=0.3125 / 16)
+            else:
+                nc.vector.tensor_scalar(b_win[t][:, :S], b_banks[pair][:, u, :], 0.3125 / 16, None, ALU.mult)
             nc.scalar.activation(pa2[pair][:, u, :], b_win[t][:].indirect(n3_t[:]), ACT.Copy)
             nc.scalar.activation(pb2[pair][:, u, :], b_win[t][:].indirect(n4_t[:]), ACT.Copy)
 
         a_banks = coded_product("a", k1_t, offs_t, nc.sync)
 
         w_raw = {}
-        for name, src in (("w2", w2), ("w1", w1)):
-            w_raw[name] = sb(name + "_raw", [P, PACK, N], F32)
+        for name, src, slot in (("w2", w2, "plane_a"), ("w1", w1, "dealt_a")):
+            w_raw[name] = sb(name + "_raw", [P, PACK, N], F32, tag=slot)
             nc.sync.dma_start(w_raw[name][:], src.rearrange("(p t) m -> p t m", t=PACK))
 
         z_grouped = sb("z_grouped", [P, S, PACK], BF16)
@@ -152,18 +158,18 @@ def tile_picked_pqjratiostdgmaxd_none_p_kernel(
 
         def b_middle(pair):
             s1, dd = work["s1", pair][:], work["dd", pair][:]
-            nc.vector.scalar_tensor_tensor(b_tile("ee", pair), s1, -9.6, b_banks[pair][:], ALU.mult, ALU.add)
+            nc.vector.scalar_tensor_tensor(b_tile("ee", pair), b_banks[pair][:], -0.625 / 16 / 1.2, s1, ALU.mult, ALU.add)
             nc.vector.tensor_tensor(b_tile("dd2", pair), dd, dd, ALU.mult)
 
         def b_spread(pair):
             s1, ee = work["s1", pair][:], work["ee", pair][:]
-            nc.vector.scalar_tensor_tensor(b_tile("ee2", pair), ee, (0.625 / 16) ** 2, ee, ALU.mult, ALU.mult)
+            nc.vector.scalar_tensor_tensor(b_tile("ee2", pair), ee, 0.140625, ee, ALU.mult, ALU.mult)
             offset[pair] = b_tile("offset", pair)
-            nc.vector.scalar_tensor_tensor(offset[pair], s1, -80.0 / 11.0, b_banks[pair][:], ALU.mult, ALU.add)
+            nc.vector.scalar_tensor_tensor(offset[pair], b_banks[pair][:], 0.6875 / 16, s1, ALU.mult, ALU.subtract)
             spread = b_tile("spread", pair)
             nc.vector.tensor_tensor(spread, work["dd2", pair][:], work["ee2", pair][:], ALU.add)
             inv[pair] = b_tile("inv", pair)
-            nc.scalar.activation(inv[pair], spread, ACT.Abs_reciprocal_sqrt, bias=0.25, scale=0.5)
+            nc.scalar.activation(inv[pair], spread, ACT.Abs_reciprocal_sqrt, bias=0.25, scale=5.12)
 
         def b_finish(pair):
             for u in range(2):
@@ -181,17 +187,22 @@ def tile_picked_pqjratiostdgmaxd_none_p_kernel(
             for u in range(2):
                 t = 2 * pair + u
                 a_win = sb("a_win%d" % t, [P, S], F32)
-                nc.vector.tensor_scalar(a_win[:], a_banks[pair][:, u, :], 0.0625, None, ALU.mult)
+                if t < AS:
+                    nc.scalar.activation(a_win[:], a_banks[pair][:, u, :], ACT.Copy, scale=0.0625)
+                else:
+                    nc.vector.tensor_scalar(a_win[:], a_banks[pair][:, u, :], 0.0625, None, ALU.mult)
                 nc.scalar.activation(pb[pair][:, u, :], a_win[:].indirect(n2_t[:]), ACT.Copy)
                 nc.scalar.activation(pa[pair][:, u, :], a_win[:].indirect(n1_t[:]), ACT.Copy)
 
-        def a_larger(pair):
+        def a_size(pair):
             size = sb("size_%d" % pair, [P, 2, W], F32)
             nc.vector.scalar_tensor_tensor(size[:], pb[pair][:], -1.0, pb[pair][:], ALU.mult, ALU.max)
-            rb = sb("rb_%d" % pair, [P, 2, W], F32)
-            nc.vector.tensor_tensor(rb[:], pa[pair][:], pb[pair][:], ALU.max)
             root[pair] = sb("root_%d" % pair, [P, 2, W], F32)
             nc.scalar.activation(root[pair][:], size[:], ACT.Abs_reciprocal_sqrt, bias=0.5)
+
+        def a_larger(pair):
+            rb = sb("rb_%d" % pair, [P, 2, W], F32)
+            nc.vector.tensor_tensor(rb[:], pa[pair][:], pb[pair][:], ALU.max)
             for u in range(2):
                 nc.scalar.activation(dt[2 * pair + u][:].indirect(n2_t[:]), rb[:, u, :], ACT.Copy)
 
@@ -203,33 +214,31 @@ def tile_picked_pqjratiostdgmaxd_none_p_kernel(
             for u in range(2):
                 nc.scalar.activation(dt[2 * pair + u][:].indirect(n1_t[:]), ra[:, u, :], ACT.Copy)
 
-        def a_round(pair):
-            for u in range(2):
-                t = 2 * pair + u
-                nc.vector.tensor_scalar(z_grouped[:, :, t], dt[t][:], gn_t[:, t : t + 1], None, ALU.mult)
+        def a_round(t):
+            nc.vector.tensor_scalar(z_grouped[:, :, t], dt[t][:], gn_t[:, t : t + 1], None, ALU.mult)
 
         def quantize(name, grouped, width):
             codes = sb(name + "_codes", [P, width], U32)
             scales = sb(name + "_scales", [P, width], U8)
-            nc.vector.quantize_mx(
-                out=codes[:].bitcast(FP8X4), scales=scales[:], in_=grouped[:].rearrange("p w t -> p (w t)")
-            )
+            nc.vector.quantize_mx(out=codes[:].bitcast(FP8X4), scales=scales[:], in_=grouped.rearrange("p w t -> p (w t)"))
             return codes, scales
 
-        def interleave(name, src, width):
-            grouped = sb(name + "_grouped", [P, width, PACK], BF16)
+        def interleave(grouped, src):
             nc.vector.tensor_copy(
-                grouped[:].rearrange("p (c i) t -> p c t i", i=4), src.rearrange("p t (c i) -> p c t i", i=4)
+                grouped.rearrange("p (c i) t -> p c t i", i=4), src.rearrange("p t (c i) -> p c t i", i=4)
             )
-            return grouped
 
         wq = {}
 
-        def weights(m):
-            cols = slice(m * P, (m + 1) * P)
-            grouped = {name: interleave("%s_%d" % (name, m), w_raw[name][:, :, cols], P) for name in ("w2", "w1")}
-            for name in ("w2", "w1"):
-                wq[name, m] = quantize("%s_%d" % (name, m), grouped[name], P)
+        w_grouped = {}
+
+        def round_weights(m):
+            w_grouped[m] = sb("w_grouped%d" % m, [P, 2 * P, PACK], BF16, tag=("", "z_grouped", "w0_codes", "w0_scales")[m])
+            for half, name in enumerate(("w2", "w1")):
+                interleave(w_grouped[m][:, half * P : (half + 1) * P, :], w_raw[name][:, :, m * P : (m + 1) * P])
+
+        def quantize_weights(m):
+            wq[m] = quantize("w%d" % m, w_grouped[m][:], 2 * P)
 
         b_sums(0)
         a_fetch(0)
@@ -237,34 +246,44 @@ def tile_picked_pqjratiostdgmaxd_none_p_kernel(
         a_fetch(1)
         b_spread(0)
         b_sums(1)
+        a_size(0)
         a_larger(0)
         b_middle(1)
-        a_larger(1)
-        b_spread(1)
         a_ratio(0)
+        a_size(1)
+        b_spread(1)
+        a_larger(1)
         a_ratio(1)
         b_finish(0)
-        weights(0)
-        b_finish(1)
-        z2_grouped = interleave("z2", z2_planes[:], S)
+        round_weights(0)
         a_round(0)
-        z2q = quantize("z2", z2_grouped, S)
+        b_finish(1)
         a_round(1)
-        zq = quantize("z", z_grouped, S)
+        quantize_weights(0)
+        z2_grouped = sb("z2_grouped", [P, S, PACK], BF16)
+        interleave(z2_grouped[:], z2_planes[:])
+        a_round(2)
+        z2q = quantize("z2", z2_grouped[:], S)
+        a_round(3)
+        zq = quantize("z", z_grouped[:], S)
 
         def h_product(m):
             bank = psum.tile([P, S], F32, name="bank_h%d" % m)
-            for first, name, act in ((True, "w2", z2q), (False, "w1", zq)):
+            for half, act in enumerate((z2q, zq)):
+                cols = slice(half * P, (half + 1) * P)
                 nc.tensor.matmul_mx(
                     out=bank[:],
-                    lhsT=wq[name, m][0][:].bitcast(FP8X4),
-                    lhsT_scale=wq[name, m][1][:],
+                    lhsT=wq[m][0][:, cols].bitcast(FP8X4),
+                    lhsT_scale=wq[m][1][:, cols],
                     rhs=act[0][:].bitcast(FP8X4),
                     rhs_scale=act[1][:],
-                    start=first,
-                    stop=not first,
+                    start=half == 0,
+                    stop=half == 1,
                 )
-            nc.vector.tensor_copy(h_win[m][:, :S], bank[:])
+            if m == 0:
+                nc.scalar.activation(h_win[m][:, :S], bank[:], ACT.Copy)
+            else:
+                nc.vector.tensor_copy(h_win[m][:, :S], bank[:])
 
         def h_finish(m, first, count, result):
             tag = "%d_%d" % (m, first)
@@ -286,7 +305,8 @@ def tile_picked_pqjratiostdgmaxd_none_p_kernel(
 
         h_product(0)
         for m in range(1, N // P):
-            weights(m)
+            round_weights(m)
+            quantize_weights(m)
             h_product(m)
         for m in range(N // P):
             rows = slice(m * P, (m + 1) * P)
@@ -296,7 +316,7 @@ def tile_picked_pqjratiostdgmaxd_none_p_kernel(
                     h_finish(m, first, H_PIECE, result)
                 nc.sync.dma_start(out[rows, :], result[:])
             else:
-                for first, count in ((0, 512), (512, 256), (768, 256)):
+                for first, count in LAST:
                     h_finish(m, first, count, result)
                     cols = slice(first // 4, (first + count) // 4)
                     nc.sync.dma_start(out[rows, cols], result[:, cols])

@@ -3,7 +3,7 @@ from contextlib import ExitStack
 import concourse.mybir as mybir
 
 K, T, S, N, G, H, W, U = 512, 1024, 256, 512, 2048, 512, 128, 1024
-FLOPS = 4 * 2 * 512 * 512 * 256
+FLOPS = 2 * (2 * K * H * S) + 2 * (2 * H * N * S)
 
 F32 = mybir.dt.float32
 BF16 = mybir.dt.bfloat16
@@ -15,14 +15,14 @@ FP8X4 = mybir.dt.float8_e4m3fn_x4
 ALU = mybir.AluOpType
 ACT = mybir.ActivationFunctionType
 
-BS = 4
-AS = 2
-LAST = ((0, 448), (448, 384), (832, 192))
 P = 128
 PACK = 4
-B_WIN = 512
-H_WIN = 528
+MEMBERS = 4
+B_WINDOW = 2 * S
 H_PIECE = 512
+H_WINDOW = H_PIECE + 16
+LAST_PIECES = ((0, 448), (448, 384), (832, 192))
+A_COPIES_ON_SCALAR = 0
 
 
 def tile_picked_pqjratiostdgmaxd_none_p_kernel(
@@ -33,8 +33,8 @@ def tile_picked_pqjratiostdgmaxd_none_p_kernel(
         keep = ctx.enter_context(tc.tile_pool(name="keep", bufs=1))
         psum = ctx.enter_context(tc.psum_pool(name="psum", bufs=1))
 
-        def sb(name, shape, dtype, tag=""):
-            return keep.tile(shape, dtype, name=name, tag=tag or name, align_bytes=64)
+        def sb(name, shape, dtype, after=""):
+            return keep.tile(shape, dtype, name=name, tag=after or name, align_bytes=64)
 
         def load_list(name, src):
             tile = keep.tile(list(src.shape), U16, name=name)
@@ -47,14 +47,14 @@ def tile_picked_pqjratiostdgmaxd_none_p_kernel(
             nc.sync.dma_start(tile[:].bitcast(I32), rows.unsqueeze(1).to_broadcast([16, 8, width // 4]))
             return tile
 
-        def load_gains(name, src, slot):
-            tile = sb(name, [P, PACK], F32, tag=slot)
-            nc.sync.dma_start(tile[:], src.rearrange("(p t) o -> p (t o)", t=PACK))
-            return tile
-
         def load_words(name, src, width):
             tile = sb(name, [P, width], I32)
-            nc.sync.dma_start(tile[:], src[0].rearrange("p n t -> p (n t)").bitcast(I32))
+            nc.sync.dma_start(tile[:], src[0].rearrange("p n r -> p (n r)").bitcast(I32))
+            return tile
+
+        def load_dealt(name, src, width, after):
+            tile = sb(name, [P, PACK, width], F32, after)
+            nc.sync.dma_start(tile[:], src.rearrange("(p t) m -> p t m", t=PACK))
             return tile
 
         k2_t = load_list("k2_t", k2)
@@ -76,21 +76,18 @@ def tile_picked_pqjratiostdgmaxd_none_p_kernel(
         warm_out = sb("warm_out", [P, 1], F32)
         nc.scalar.activation(warm_out[:], warm_in[:], ACT.Abs_reciprocal_sqrt, bias=0.25, scale=0.5)
 
-        b_win = [sb("b_win%d" % t, [P, B_WIN], F32) for t in range(PACK)]
-        h_win = [sb("h_win%d" % m, [P, H_WIN], F32) for m in range(N // P)]
-
         def coded_product(name, k_list, x_list, queue):
             d_bytes = sb("d_bytes_" + name, [P, H], U8)
             nc.vector.tensor_copy(d_bytes[:], d_sc[:].indirect(k_list[:]))
             x_bytes = sb("x_bytes_" + name, [P, S], U8)
             nc.vector.tensor_copy(x_bytes[:], x_sc[:].indirect(x_list[:]))
-            plane = sb("plane_" + name, [P, H + S], U8)
+            scales = sb("scales_" + name, [P, H + S], U8)
             nc.vector.tensor_copy(
-                plane[:, :H].rearrange("p (t m) -> p m t", t=PACK), d_bytes[:].rearrange("p (m t) -> p m t", t=PACK)
+                scales[:, :H].rearrange("p (t m) -> p m t", t=PACK), d_bytes[:].rearrange("p (m t) -> p m t", t=PACK)
             )
-            nc.vector.tensor_copy(plane[:, H:].bitcast(I32), x_bytes[:].bitcast(I32))
+            nc.vector.tensor_copy(scales[:, H:].bitcast(I32), x_bytes[:].bitcast(I32))
             for c in range(1, 4):
-                queue.dma_start(plane[c:P:32, :].bitcast(I32), plane[8 * c : P : 32, :].bitcast(I32))
+                queue.dma_start(scales[c:P:32, :].bitcast(I32), scales[8 * c : P : 32, :].bitcast(I32))
 
             d_codes = sb("d_codes_" + name, [P, H], U32)
             nc.vector.tensor_copy(d_codes[:], d_wd[:].bitcast(U32).indirect(k_list[:]))
@@ -102,143 +99,136 @@ def tile_picked_pqjratiostdgmaxd_none_p_kernel(
                 d_codes[:].bitcast(I32).rearrange("p (c i t) -> p c t i", t=PACK, i=4),
             )
             banks = []
-            for pair in range(2):
-                bank = psum.tile([P, 2, S], F32, name="bank_%s%d" % (name, pair))
-                for u in range(2):
-                    cols = slice((2 * pair + u) * P, (2 * pair + u + 1) * P)
-                    nc.tensor.matmul_mx(
-                        out=bank[:, u, :],
-                        lhsT=dealt[:, cols].bitcast(FP8X4),
-                        lhsT_scale=plane[:, cols],
-                        rhs=x_codes[:].bitcast(FP8X4),
-                        rhs_scale=plane[:, H:],
-                        start=True,
-                        stop=True,
-                    )
+            for t in range(PACK):
+                bank = psum.tile([P, S], F32, name="bank_%s%d" % (name, t))
+                cols = slice(t * P, (t + 1) * P)
+                nc.tensor.matmul_mx(
+                    out=bank[:],
+                    lhsT=dealt[:, cols].bitcast(FP8X4),
+                    lhsT_scale=scales[:, cols],
+                    rhs=x_codes[:].bitcast(FP8X4),
+                    rhs_scale=scales[:, H:],
+                    start=True,
+                    stop=True,
+                )
                 banks.append(bank)
             return banks
 
         b_banks = coded_product("b", k2_t, two_t, nc.scalar)
-
-        gm_t = load_gains("gm_t", gm, "x_codes_b")
-        gn_t = load_gains("gn_t", gn, "dealt_b")
+        gm_t = load_dealt("gm_t", gm, 1, "x_codes_b")
+        gn_t = load_dealt("gn_t", gn, 1, "dealt_b")
 
         pa2 = [sb("pa2_%d" % pair, [P, 2, S], F32) for pair in range(2)]
         pb2 = [sb("pb2_%d" % pair, [P, 2, S], F32) for pair in range(2)]
         for t in range(PACK):
             pair, u = divmod(t, 2)
-            if t < BS:
-                nc.scalar.activation(b_win[t][:, :S], b_banks[pair][:, u, :], ACT.Copy, scale=0.3125 / 16)
-            else:
-                nc.vector.tensor_scalar(b_win[t][:, :S], b_banks[pair][:, u, :], 0.3125 / 16, None, ALU.mult)
-            nc.scalar.activation(pa2[pair][:, u, :], b_win[t][:].indirect(n3_t[:]), ACT.Copy)
-            nc.scalar.activation(pb2[pair][:, u, :], b_win[t][:].indirect(n4_t[:]), ACT.Copy)
+            b_win = sb("b_win%d" % t, [P, B_WINDOW], F32)
+            nc.scalar.activation(b_win[:, :S], b_banks[t][:], ACT.Copy, scale=0.3125 / 16)
+            nc.scalar.activation(pa2[pair][:, u, :], b_win[:].indirect(n3_t[:]), ACT.Copy)
+            nc.scalar.activation(pb2[pair][:, u, :], b_win[:].indirect(n4_t[:]), ACT.Copy)
 
         a_banks = coded_product("a", k1_t, offs_t, nc.sync)
-
-        w_raw = {}
-        for name, src, slot in (("w2", w2, "plane_a"), ("w1", w1, "dealt_a")):
-            w_raw[name] = sb(name + "_raw", [P, PACK, N], F32, tag=slot)
-            nc.sync.dma_start(w_raw[name][:], src.rearrange("(p t) m -> p t m", t=PACK))
-
-        z_grouped = sb("z_grouped", [P, S, PACK], BF16)
-        z2_planes = sb("z2_planes", [P, PACK, S], BF16)
-        offset = {}
-        inv = {}
+        w2_raw = load_dealt("w2_raw", w2, N, "scales_a")
+        w1_raw = load_dealt("w1_raw", w1, N, "dealt_a")
 
         work = {}
 
-        def b_tile(name, pair):
-            work[name, pair] = sb("%s_%d" % (name, pair), [P, 2, S], F32)
+        def pair_tile(name, pair, width, after=""):
+            work[name, pair] = sb("%s_%d" % (name, pair), [P, 2, width], F32, after)
             return work[name, pair][:]
 
         def b_sums(pair):
-            nc.vector.tensor_tensor(b_tile("s1", pair), pa2[pair][:], pb2[pair][:], ALU.add)
-            nc.vector.tensor_tensor(b_tile("dd", pair), pa2[pair][:], pb2[pair][:], ALU.subtract)
+            nc.vector.tensor_tensor(pair_tile("total", pair, S), pa2[pair][:], pb2[pair][:], ALU.add)
+            nc.vector.tensor_tensor(pair_tile("diff", pair, S), pa2[pair][:], pb2[pair][:], ALU.subtract)
 
         def b_middle(pair):
-            s1, dd = work["s1", pair][:], work["dd", pair][:]
-            nc.vector.scalar_tensor_tensor(b_tile("ee", pair), b_banks[pair][:], -0.625 / 16 / 1.2, s1, ALU.mult, ALU.add)
-            nc.vector.tensor_tensor(b_tile("dd2", pair), dd, dd, ALU.mult)
+            total, diff, mid = work["total", pair], work["diff", pair], pair_tile("mid", pair, S)
+            for u in range(2):
+                nc.vector.scalar_tensor_tensor(
+                    mid[:, u, :], b_banks[2 * pair + u][:], -0.625 / 16 / 1.2, total[:, u, :], ALU.mult, ALU.add
+                )
+            nc.vector.tensor_tensor(pair_tile("diff_sq", pair, S), diff[:], diff[:], ALU.mult)
 
         def b_spread(pair):
-            s1, ee = work["s1", pair][:], work["ee", pair][:]
-            nc.vector.scalar_tensor_tensor(b_tile("ee2", pair), ee, 0.140625, ee, ALU.mult, ALU.mult)
-            offset[pair] = b_tile("offset", pair)
-            nc.vector.scalar_tensor_tensor(offset[pair], b_banks[pair][:], 0.6875 / 16, s1, ALU.mult, ALU.subtract)
-            spread = b_tile("spread", pair)
-            nc.vector.tensor_tensor(spread, work["dd2", pair][:], work["ee2", pair][:], ALU.add)
-            inv[pair] = b_tile("inv", pair)
-            nc.scalar.activation(inv[pair], spread, ACT.Abs_reciprocal_sqrt, bias=0.25, scale=5.12)
+            total, mid = work["total", pair], work["mid", pair][:]
+            nc.vector.scalar_tensor_tensor(pair_tile("mid_sq", pair, S), mid, 0.140625, mid, ALU.mult, ALU.mult)
+            centred = pair_tile("centred", pair, S)
+            for u in range(2):
+                nc.vector.scalar_tensor_tensor(
+                    centred[:, u, :], b_banks[2 * pair + u][:], 0.6875 / 16, total[:, u, :], ALU.mult, ALU.subtract
+                )
+            spread = pair_tile("spread", pair, S)
+            nc.vector.tensor_tensor(spread, work["diff_sq", pair][:], work["mid_sq", pair][:], ALU.add)
+            inv = pair_tile("inv", pair, S)
+            nc.scalar.activation(inv, spread, ACT.Abs_reciprocal_sqrt, bias=0.25, scale=5.12)
+
+        z2_tiles = sb("z2_tiles", [P, PACK, S], BF16)
 
         def b_finish(pair):
+            centred, inv = work["centred", pair], work["inv", pair]
             for u in range(2):
                 t = 2 * pair + u
                 nc.vector.scalar_tensor_tensor(
-                    z2_planes[:, t, :], offset[pair][:, u, :], gm_t[:, t : t + 1], inv[pair][:, u, :], ALU.mult, ALU.mult
+                    z2_tiles[:, t, :], centred[:, u, :], gm_t[:, t, :], inv[:, u, :], ALU.mult, ALU.mult
                 )
 
-        pa = [sb("pa_%d" % pair, [P, 2, W], F32) for pair in range(2)]
-        pb = [sb("pb_%d" % pair, [P, 2, W], F32) for pair in range(2)]
         dt = [sb("dt_%d" % t, [P, S], F32) for t in range(PACK)]
-        root = {}
 
         def a_fetch(pair):
+            pa, pb = pair_tile("pa", pair, W), pair_tile("pb", pair, W)
             for u in range(2):
                 t = 2 * pair + u
                 a_win = sb("a_win%d" % t, [P, S], F32)
-                if t < AS:
-                    nc.scalar.activation(a_win[:], a_banks[pair][:, u, :], ACT.Copy, scale=0.0625)
+                if t < A_COPIES_ON_SCALAR:
+                    nc.scalar.activation(a_win[:], a_banks[t][:], ACT.Copy, scale=0.0625)
                 else:
-                    nc.vector.tensor_scalar(a_win[:], a_banks[pair][:, u, :], 0.0625, None, ALU.mult)
-                nc.scalar.activation(pb[pair][:, u, :], a_win[:].indirect(n2_t[:]), ACT.Copy)
-                nc.scalar.activation(pa[pair][:, u, :], a_win[:].indirect(n1_t[:]), ACT.Copy)
+                    nc.vector.tensor_scalar(a_win[:], a_banks[t][:], 0.0625, None, ALU.mult)
+                nc.scalar.activation(pb[:, u, :], a_win[:].indirect(n2_t[:]), ACT.Copy)
+                nc.scalar.activation(pa[:, u, :], a_win[:].indirect(n1_t[:]), ACT.Copy)
 
         def a_size(pair):
-            size = sb("size_%d" % pair, [P, 2, W], F32)
-            nc.vector.scalar_tensor_tensor(size[:], pb[pair][:], -1.0, pb[pair][:], ALU.mult, ALU.max)
-            root[pair] = sb("root_%d" % pair, [P, 2, W], F32)
-            nc.scalar.activation(root[pair][:], size[:], ACT.Abs_reciprocal_sqrt, bias=0.5)
+            pb, size = work["pb", pair][:], pair_tile("size", pair, W)
+            nc.vector.scalar_tensor_tensor(size, pb, -1.0, pb, ALU.mult, ALU.max)
+            nc.scalar.activation(pair_tile("root", pair, W), size, ACT.Abs_reciprocal_sqrt, bias=0.5)
 
         def a_larger(pair):
-            rb = sb("rb_%d" % pair, [P, 2, W], F32)
-            nc.vector.tensor_tensor(rb[:], pa[pair][:], pb[pair][:], ALU.max)
+            rb = pair_tile("rb", pair, W)
+            nc.vector.tensor_tensor(rb, work["pa", pair][:], work["pb", pair][:], ALU.max)
             for u in range(2):
                 nc.scalar.activation(dt[2 * pair + u][:].indirect(n2_t[:]), rb[:, u, :], ACT.Copy)
 
         def a_ratio(pair):
-            half = sb("half_%d" % pair, [P, 2, W], F32)
-            nc.vector.tensor_tensor(half[:], pa[pair][:], root[pair][:], ALU.mult)
-            ra = sb("ra_%d" % pair, [P, 2, W], F32)
-            nc.vector.tensor_tensor(ra[:], half[:], root[pair][:], ALU.mult)
+            root, once, ra = work["root", pair][:], pair_tile("once", pair, W), pair_tile("ra", pair, W)
+            nc.vector.tensor_tensor(once, work["pa", pair][:], root, ALU.mult)
+            nc.vector.tensor_tensor(ra, once, root, ALU.mult)
             for u in range(2):
                 nc.scalar.activation(dt[2 * pair + u][:].indirect(n1_t[:]), ra[:, u, :], ACT.Copy)
 
+        z_grouped = sb("z_grouped", [P, S, PACK], BF16)
+
         def a_round(t):
-            nc.vector.tensor_scalar(z_grouped[:, :, t], dt[t][:], gn_t[:, t : t + 1], None, ALU.mult)
+            nc.vector.tensor_scalar(z_grouped[:, :, t], dt[t][:], gn_t[:, t, :], None, ALU.mult)
+
+        def interleave(grouped, tiles):
+            nc.vector.tensor_copy(
+                grouped.rearrange("p (c i) t -> p c t i", i=4), tiles.rearrange("p t (c i) -> p c t i", i=4)
+            )
 
         def quantize(name, grouped, width):
             codes = sb(name + "_codes", [P, width], U32)
             scales = sb(name + "_scales", [P, width], U8)
-            nc.vector.quantize_mx(out=codes[:].bitcast(FP8X4), scales=scales[:], in_=grouped.rearrange("p w t -> p (w t)"))
+            nc.vector.quantize_mx(
+                out=codes[:].bitcast(FP8X4), scales=scales[:], in_=grouped[:].rearrange("p j t -> p (j t)")
+            )
             return codes, scales
 
-        def interleave(grouped, src):
-            nc.vector.tensor_copy(
-                grouped.rearrange("p (c i) t -> p c t i", i=4), src.rearrange("p t (c i) -> p c t i", i=4)
-            )
-
-        wq = {}
-
+        w_after = ("", "z_grouped", "w0_codes", "w0_scales")
         w_grouped = {}
 
         def round_weights(m):
-            w_grouped[m] = sb("w_grouped%d" % m, [P, 2 * P, PACK], BF16, tag=("", "z_grouped", "w0_codes", "w0_scales")[m])
-            for half, name in enumerate(("w2", "w1")):
-                interleave(w_grouped[m][:, half * P : (half + 1) * P, :], w_raw[name][:, :, m * P : (m + 1) * P])
-
-        def quantize_weights(m):
-            wq[m] = quantize("w%d" % m, w_grouped[m][:], 2 * P)
+            w_grouped[m] = sb("w_grouped%d" % m, [P, 2 * P, PACK], BF16, w_after[m])
+            for half, raw in enumerate((w2_raw, w1_raw)):
+                interleave(w_grouped[m][:, half * P : (half + 1) * P, :], raw[:, :, m * P : (m + 1) * P])
 
         b_sums(0)
         a_fetch(0)
@@ -259,24 +249,26 @@ def tile_picked_pqjratiostdgmaxd_none_p_kernel(
         a_round(0)
         b_finish(1)
         a_round(1)
-        quantize_weights(0)
+        first_weights = quantize("w0", w_grouped[0], 2 * P)
         z2_grouped = sb("z2_grouped", [P, S, PACK], BF16)
-        interleave(z2_grouped[:], z2_planes[:])
+        interleave(z2_grouped[:], z2_tiles[:])
         a_round(2)
-        z2q = quantize("z2", z2_grouped[:], S)
+        z2q = quantize("z2", z2_grouped, S)
         a_round(3)
-        zq = quantize("z", z_grouped[:], S)
+        zq = quantize("z", z_grouped, S)
 
-        def h_product(m):
-            bank = psum.tile([P, S], F32, name="bank_h%d" % m)
-            for half, act in enumerate((z2q, zq)):
+        h_win = [sb("h_win%d" % m, [P, H_WINDOW], F32) for m in range(N // P)]
+
+        def h_product(m, weights):
+            bank = psum.tile([P, S], F32, name="bank_h%d" % m, tag="bank_a%d" % m)
+            for half, (codes, scales) in enumerate((z2q, zq)):
                 cols = slice(half * P, (half + 1) * P)
                 nc.tensor.matmul_mx(
                     out=bank[:],
-                    lhsT=wq[m][0][:, cols].bitcast(FP8X4),
-                    lhsT_scale=wq[m][1][:, cols],
-                    rhs=act[0][:].bitcast(FP8X4),
-                    rhs_scale=act[1][:],
+                    lhsT=weights[0][:, cols].bitcast(FP8X4),
+                    lhsT_scale=weights[1][:, cols],
+                    rhs=codes[:].bitcast(FP8X4),
+                    rhs_scale=scales[:],
                     start=half == 0,
                     stop=half == 1,
                 )
@@ -285,38 +277,27 @@ def tile_picked_pqjratiostdgmaxd_none_p_kernel(
             else:
                 nc.vector.tensor_copy(h_win[m][:, :S], bank[:])
 
-        def h_finish(m, first, count, result):
-            tag = "%d_%d" % (m, first)
-            cols = slice(first // 4, (first + count) // 4)
-            members = sb("members_" + tag, [P, count // 4, 4], F32)
+        def h_finish(m, first, count, engine):
+            name = "%d_%d" % (m, first)
+            cols = slice(first // MEMBERS, (first + count) // MEMBERS)
+            members = sb("members_" + name, [P, count // MEMBERS, MEMBERS], F32)
             nc.scalar.activation(
-                members[:].rearrange("p j t -> p (j t)"),
+                members[:].rearrange("p j e -> p (j e)"),
                 h_win[m][:].indirect(n5_t[:, first // 16 : (first + count) // 16]),
                 ACT.Copy,
             )
-            largest = sb("largest_" + tag, [P, count // 4], F32)
-            if count == H_PIECE:
-                pairs = sb("pairs_" + tag, [P, count // 4, 2], F32)
-                nc.vector.tensor_tensor(pairs[:], members[:, :, 0:2], members[:, :, 2:4], ALU.max)
-                nc.vector.tensor_tensor(largest[:], pairs[:, :, 0], pairs[:, :, 1], ALU.max)
-            else:
-                nc.vector.tensor_reduce(largest[:], members[:], mybir.AxisListType.X, ALU.max)
-            nc.vector.tensor_tensor(result[:, cols], h_win[m][:, cols], largest[:], ALU.subtract)
+            largest = sb("largest_" + name, [P, count // MEMBERS], F32)
+            nc.vector.tensor_reduce(largest[:], members[:], mybir.AxisListType.X, ALU.max)
+            result = sb("result_" + name, [P, count // MEMBERS], F32)
+            engine.tensor_tensor(result[:], h_win[m][:, cols], largest[:], ALU.subtract)
+            nc.sync.dma_start(out[m * P : (m + 1) * P, cols], result[:])
 
-        h_product(0)
+        h_product(0, first_weights)
         for m in range(1, N // P):
             round_weights(m)
-            quantize_weights(m)
-            h_product(m)
-        for m in range(N // P):
-            rows = slice(m * P, (m + 1) * P)
-            result = sb("result_%d" % m, [P, S], F32)
-            if m + 1 < N // P:
-                for first in range(0, U, H_PIECE):
-                    h_finish(m, first, H_PIECE, result)
-                nc.sync.dma_start(out[rows, :], result[:])
-            else:
-                for first, count in LAST:
-                    h_finish(m, first, count, result)
-                    cols = slice(first // 4, (first + count) // 4)
-                    nc.sync.dma_start(out[rows, cols], result[:, cols])
+            h_product(m, quantize("w%d" % m, w_grouped[m], 2 * P))
+        for m in range(N // P - 1):
+            for first in range(0, U, H_PIECE):
+                h_finish(m, first, H_PIECE, nc.gpsimd)
+        for first, count in LAST_PIECES:
+            h_finish(N // P - 1, first, count, nc.vector if first + count == U else nc.gpsimd)

from contextlib import ExitStack

import concourse.mybir as mybir

K, T, S, N, G, H, W, U = 512, 1024, 256, 512, 2048, 512, 128, 1024
FLOPS = 2 * (2 * K * H * S) + 2 * (2 * H * N * S)

F32 = mybir.dt.float32
BF16 = mybir.dt.bfloat16
I32 = mybir.dt.int32
U32 = mybir.dt.uint32
U16 = mybir.dt.uint16
U8 = mybir.dt.uint8
FP8X4 = mybir.dt.float8_e4m3fn_x4
ALU = mybir.AluOpType
ACT = mybir.ActivationFunctionType

P = 128
PACK = 4
MEMBERS = 4
B_WINDOW = 2 * S
H_PIECE = 512
H_WINDOW = H_PIECE + 16
LAST_PIECES = ((0, 448), (448, 384), (832, 192))
A_COPIES_ON_SCALAR = 0


def tile_picked_pqjratiostdgmaxd_none_p_kernel(
    tc, x_words, x_scales, d_words, d_scales, gn, gm, w1, w2, offs, k1, two, k2, n1, n2, n3, n4, n5, out
):
    nc = tc.nc
    with ExitStack() as ctx:
        keep = ctx.enter_context(tc.tile_pool(name="keep", bufs=1))
        psum = ctx.enter_context(tc.psum_pool(name="psum", bufs=1))

        def sb(name, shape, dtype, after=""):
            return keep.tile(shape, dtype, name=name, tag=after or name, align_bytes=64)

        def load_list(name, src):
            tile = keep.tile(list(src.shape), U16, name=name)
            nc.sync.dma_start(tile[:], src)
            return tile

        def load_scale_rows(name, src, width):
            tile = sb(name, [P, width], U8)
            rows = src[0].bitcast(I32)
            nc.sync.dma_start(tile[:].bitcast(I32), rows.unsqueeze(1).to_broadcast([16, 8, width // 4]))
            return tile

        def load_words(name, src, width):
            tile = sb(name, [P, width], I32)
            nc.sync.dma_start(tile[:], src[0].rearrange("p n r -> p (n r)").bitcast(I32))
            return tile

        def load_dealt(name, src, width, after):
            tile = sb(name, [P, PACK, width], F32, after)
            nc.sync.dma_start(tile[:], src.rearrange("(p t) m -> p t m", t=PACK))
            return tile

        k2_t = load_list("k2_t", k2)
        d_sc = load_scale_rows("d_sc", d_scales, G)
        two_t = load_list("two_t", two)
        x_sc = load_scale_rows("x_sc", x_scales, T)
        n3_t = load_list("n3_t", n3)
        n4_t = load_list("n4_t", n4)
        n1_t = load_list("n1_t", n1)
        d_wd = load_words("d_wd", d_words, G)
        x_wd = load_words("x_wd", x_words, T)
        k1_t = load_list("k1_t", k1)
        offs_t = load_list("offs_t", offs)
        n2_t = load_list("n2_t", n2)
        n5_t = load_list("n5_t", n5)

        warm_in = sb("warm_in", [P, 1], F32)
        nc.vector.memset(warm_in[:], 1.0)
        warm_out = sb("warm_out", [P, 1], F32)
        nc.scalar.activation(warm_out[:], warm_in[:], ACT.Abs_reciprocal_sqrt, bias=0.25, scale=0.5)

        def coded_product(name, k_list, x_list, queue):
            d_bytes = sb("d_bytes_" + name, [P, H], U8)
            nc.vector.tensor_copy(d_bytes[:], d_sc[:].indirect(k_list[:]))
            x_bytes = sb("x_bytes_" + name, [P, S], U8)
            nc.vector.tensor_copy(x_bytes[:], x_sc[:].indirect(x_list[:]))
            scales = sb("scales_" + name, [P, H + S], U8)
            nc.vector.tensor_copy(
                scales[:, :H].rearrange("p (t m) -> p m t", t=PACK), d_bytes[:].rearrange("p (m t) -> p m t", t=PACK)
            )
            nc.vector.tensor_copy(scales[:, H:].bitcast(I32), x_bytes[:].bitcast(I32))
            for c in range(1, 4):
                queue.dma_start(scales[c:P:32, :].bitcast(I32), scales[8 * c : P : 32, :].bitcast(I32))

            d_codes = sb("d_codes_" + name, [P, H], U32)
            nc.vector.tensor_copy(d_codes[:], d_wd[:].bitcast(U32).indirect(k_list[:]))
            x_codes = sb("x_codes_" + name, [P, S], U32)
            nc.vector.tensor_copy(x_codes[:], x_wd[:].bitcast(U32).indirect(x_list[:]))
            dealt = sb("dealt_" + name, [P, H], U32)
            nc.vector.tensor_copy(
                dealt[:].bitcast(I32).rearrange("p (t c i) -> p c t i", t=PACK, i=4),
                d_codes[:].bitcast(I32).rearrange("p (c i t) -> p c t i", t=PACK, i=4),
            )
            banks = []
            for t in range(PACK):
                bank = psum.tile([P, S], F32, name="bank_%s%d" % (name, t))
                cols = slice(t * P, (t + 1) * P)
                nc.tensor.matmul_mx(
                    out=bank[:],
                    lhsT=dealt[:, cols].bitcast(FP8X4),
                    lhsT_scale=scales[:, cols],
                    rhs=x_codes[:].bitcast(FP8X4),
                    rhs_scale=scales[:, H:],
                    start=True,
                    stop=True,
                )
                banks.append(bank)
            return banks

        b_banks = coded_product("b", k2_t, two_t, nc.scalar)
        gm_t = load_dealt("gm_t", gm, 1, "x_codes_b")
        gn_t = load_dealt("gn_t", gn, 1, "dealt_b")

        pa2 = [sb("pa2_%d" % pair, [P, 2, S], F32) for pair in range(2)]
        pb2 = [sb("pb2_%d" % pair, [P, 2, S], F32) for pair in range(2)]
        for t in range(PACK):
            pair, u = divmod(t, 2)
            b_win = sb("b_win%d" % t, [P, B_WINDOW], F32)
            nc.scalar.activation(b_win[:, :S], b_banks[t][:], ACT.Copy, scale=0.3125 / 16)
            nc.scalar.activation(pa2[pair][:, u, :], b_win[:].indirect(n3_t[:]), ACT.Copy)
            nc.scalar.activation(pb2[pair][:, u, :], b_win[:].indirect(n4_t[:]), ACT.Copy)

        a_banks = coded_product("a", k1_t, offs_t, nc.sync)
        w2_raw = load_dealt("w2_raw", w2, N, "scales_a")
        w1_raw = load_dealt("w1_raw", w1, N, "dealt_a")

        work = {}

        def pair_tile(name, pair, width, after=""):
            work[name, pair] = sb("%s_%d" % (name, pair), [P, 2, width], F32, after)
            return work[name, pair][:]

        def b_sums(pair):
            nc.vector.tensor_tensor(pair_tile("total", pair, S), pa2[pair][:], pb2[pair][:], ALU.add)
            nc.vector.tensor_tensor(pair_tile("diff", pair, S), pa2[pair][:], pb2[pair][:], ALU.subtract)

        def b_middle(pair):
            total, diff, mid = work["total", pair], work["diff", pair], pair_tile("mid", pair, S)
            for u in range(2):
                nc.vector.scalar_tensor_tensor(
                    mid[:, u, :], b_banks[2 * pair + u][:], -0.625 / 16 / 1.2, total[:, u, :], ALU.mult, ALU.add
                )
            nc.vector.tensor_tensor(pair_tile("diff_sq", pair, S), diff[:], diff[:], ALU.mult)

        def b_spread(pair):
            total, mid = work["total", pair], work["mid", pair][:]
            nc.vector.scalar_tensor_tensor(pair_tile("mid_sq", pair, S), mid, 0.140625, mid, ALU.mult, ALU.mult)
            centred = pair_tile("centred", pair, S)
            for u in range(2):
                nc.vector.scalar_tensor_tensor(
                    centred[:, u, :], b_banks[2 * pair + u][:], 0.6875 / 16, total[:, u, :], ALU.mult, ALU.subtract
                )
            spread = pair_tile("spread", pair, S)
            nc.vector.tensor_tensor(spread, work["diff_sq", pair][:], work["mid_sq", pair][:], ALU.add)
            inv = pair_tile("inv", pair, S)
            nc.scalar.activation(inv, spread, ACT.Abs_reciprocal_sqrt, bias=0.25, scale=5.12)

        z2_tiles = sb("z2_tiles", [P, PACK, S], BF16)

        def b_finish(pair):
            centred, inv = work["centred", pair], work["inv", pair]
            for u in range(2):
                t = 2 * pair + u
                nc.vector.scalar_tensor_tensor(
                    z2_tiles[:, t, :], centred[:, u, :], gm_t[:, t, :], inv[:, u, :], ALU.mult, ALU.mult
                )

        dt = [sb("dt_%d" % t, [P, S], F32) for t in range(PACK)]

        def a_fetch(pair):
            pa, pb = pair_tile("pa", pair, W), pair_tile("pb", pair, W)
            for u in range(2):
                t = 2 * pair + u
                a_win = sb("a_win%d" % t, [P, S], F32)
                if t < A_COPIES_ON_SCALAR:
                    nc.scalar.activation(a_win[:], a_banks[t][:], ACT.Copy, scale=0.0625)
                else:
                    nc.vector.tensor_scalar(a_win[:], a_banks[t][:], 0.0625, None, ALU.mult)
                nc.scalar.activation(pb[:, u, :], a_win[:].indirect(n2_t[:]), ACT.Copy)
                nc.scalar.activation(pa[:, u, :], a_win[:].indirect(n1_t[:]), ACT.Copy)

        def a_size(pair):
            pb, size = work["pb", pair][:], pair_tile("size", pair, W)
            nc.vector.scalar_tensor_tensor(size, pb, -1.0, pb, ALU.mult, ALU.max)
            nc.scalar.activation(pair_tile("root", pair, W), size, ACT.Abs_reciprocal_sqrt, bias=0.5)

        def a_larger(pair):
            rb = pair_tile("rb", pair, W)
            nc.vector.tensor_tensor(rb, work["pa", pair][:], work["pb", pair][:], ALU.max)
            for u in range(2):
                nc.scalar.activation(dt[2 * pair + u][:].indirect(n2_t[:]), rb[:, u, :], ACT.Copy)

        def a_ratio(pair):
            root, once, ra = work["root", pair][:], pair_tile("once", pair, W), pair_tile("ra", pair, W)
            nc.vector.tensor_tensor(once, work["pa", pair][:], root, ALU.mult)
            nc.vector.tensor_tensor(ra, once, root, ALU.mult)
            for u in range(2):
                nc.scalar.activation(dt[2 * pair + u][:].indirect(n1_t[:]), ra[:, u, :], ACT.Copy)

        z_grouped = sb("z_grouped", [P, S, PACK], BF16)

        def a_round(t):
            nc.vector.tensor_scalar(z_grouped[:, :, t], dt[t][:], gn_t[:, t, :], None, ALU.mult)

        def interleave(grouped, tiles):
            nc.vector.tensor_copy(
                grouped.rearrange("p (c i) t -> p c t i", i=4), tiles.rearrange("p t (c i) -> p c t i", i=4)
            )

        def quantize(name, grouped, width):
            codes = sb(name + "_codes", [P, width], U32)
            scales = sb(name + "_scales", [P, width], U8)
            nc.vector.quantize_mx(
                out=codes[:].bitcast(FP8X4), scales=scales[:], in_=grouped[:].rearrange("p j t -> p (j t)")
            )
            return codes, scales

        w_after = ("", "z_grouped", "w0_codes", "w0_scales")
        w_grouped = {}

        def round_weights(m):
            w_grouped[m] = sb("w_grouped%d" % m, [P, 2 * P, PACK], BF16, w_after[m])
            for half, raw in enumerate((w2_raw, w1_raw)):
                interleave(w_grouped[m][:, half * P : (half + 1) * P, :], raw[:, :, m * P : (m + 1) * P])

        b_sums(0)
        a_fetch(0)
        b_middle(0)
        a_fetch(1)
        b_spread(0)
        b_sums(1)
        a_size(0)
        a_larger(0)
        b_middle(1)
        a_ratio(0)
        a_size(1)
        b_spread(1)
        a_larger(1)
        a_ratio(1)
        b_finish(0)
        round_weights(0)
        a_round(0)
        b_finish(1)
        a_round(1)
        first_weights = quantize("w0", w_grouped[0], 2 * P)
        z2_grouped = sb("z2_grouped", [P, S, PACK], BF16)
        interleave(z2_grouped[:], z2_tiles[:])
        a_round(2)
        z2q = quantize("z2", z2_grouped, S)
        a_round(3)
        zq = quantize("z", z_grouped, S)

        h_win = [sb("h_win%d" % m, [P, H_WINDOW], F32) for m in range(N // P)]

        def h_product(m, weights):
            bank = psum.tile([P, S], F32, name="bank_h%d" % m, tag="bank_a%d" % m)
            for half, (codes, scales) in enumerate((z2q, zq)):
                cols = slice(half * P, (half + 1) * P)
                nc.tensor.matmul_mx(
                    out=bank[:],
                    lhsT=weights[0][:, cols].bitcast(FP8X4),
                    lhsT_scale=weights[1][:, cols],
                    rhs=codes[:].bitcast(FP8X4),
                    rhs_scale=scales[:],
                    start=half == 0,
                    stop=half == 1,
                )
            if m == 0:
                nc.scalar.activation(h_win[m][:, :S], bank[:], ACT.Copy)
            else:
                nc.vector.tensor_copy(h_win[m][:, :S], bank[:])

        def h_finish(m, first, count, engine):
            name = "%d_%d" % (m, first)
            cols = slice(first // MEMBERS, (first + count) // MEMBERS)
            members = sb("members_" + name, [P, count // MEMBERS, MEMBERS], F32)
            nc.scalar.activation(
                members[:].rearrange("p j e -> p (j e)"),
                h_win[m][:].indirect(n5_t[:, first // 16 : (first + count) // 16]),
                ACT.Copy,
            )
            largest = sb("largest_" + name, [P, count // MEMBERS], F32)
            nc.vector.tensor_reduce(largest[:], members[:], mybir.AxisListType.X, ALU.max)
            result = sb("result_" + name, [P, count // MEMBERS], F32)
            engine.tensor_tensor(result[:], h_win[m][:, cols], largest[:], ALU.subtract)
            nc.sync.dma_start(out[m * P : (m + 1) * P, cols], result[:])

        h_product(0, first_weights)
        for m in range(1, N // P):
            round_weights(m)
            h_product(m, quantize("w%d" % m, w_grouped[m], 2 * P))
        for m in range(N // P - 1):
            for first in range(0, U, H_PIECE):
                h_finish(m, first, H_PIECE, nc.gpsimd)
        for first, count in LAST_PIECES:
            h_finish(N // P - 1, first, count, nc.vector if first + count == U else nc.gpsimd)
